import numpy as np, ml_dtypes
CORES = [36,164,52,180,100,228,116,244]
N = 8
import mx_ref
BF = ml_dtypes.bfloat16
def entries(a):
    return np.ascontiguousarray(a.T).reshape(-1)
def table(e):
    return np.ascontiguousarray(np.reshape(e, (-1, 16)).T).astype(np.int32)
def f(rng, *shape):
    return mx_ref.flush((rng.standard_normal(shape, dtype=np.float32) * np.exp2(rng.integers(-2, 3, shape[:-1] + (1,)))).astype(BF))
def wide(rng, *shape, cols=0):
    v = rng.standard_normal(shape, dtype=np.float32) * np.exp2(rng.integers(-12, 13, shape)).astype(np.float32)
    if cols: v *= np.repeat(np.exp2(rng.integers(-cols, cols + 1, shape[:-2] + (1, shape[-1] // 4))) * (rng.random(shape[:-2] + (1, shape[-1] // 4)) > 0.0625), 4, axis=-1).astype(np.float32)
    return mx_ref.flush(v.astype(BF))
T, CAPP, OC, UN = 128, 16, 56, 32
HOST = [0 if c < 128 else 1 for c in CORES]
def term(a, B):
    return np.stack([mx_ref.matmul(mx_ref.quantize(a[:, 512 * i:512 * i + 512]), B) for i in range(4)], axis=2).reshape(128, -1)
def padded(e, k):
    return table(np.concatenate([e, np.full(k - len(e), -1)]))
def lists(rng, fixed=False, blocks=False, plain=False, short=False):
    own = [[[] for d in range(N)] for r in range(N)]
    union = np.full((N, 2, UN), -1)
    for d in range(N):
        half = np.arange(OC) if blocks else rng.permutation(OC)
        ext = [rng.choice(half[(1 - g) * (OC // 2):(2 - g) * (OC // 2)], UN - OC // 2, replace=False) for g in range(2)]
        low = int(rng.integers(0, 2)) if short else -1
        for g in range(2):
            R = [r for r in range(N) if HOST[r] == g]
            mine = list(half[g * (OC // 2):(g + 1) * (OC // 2)]) + list(ext[g])
            p = rng.permutation(len(R)); named = [set() for _ in mine]
            for k in range(CAPP):
                if not fixed: p = rng.permutation(len(R))
                for i in range(len(R) // 2): named[k * (len(R) // 2) + i] = {R[p[2 * i]], R[p[2 * i + 1]]}
            if g == low:
                both = [j for j in range(UN) if j >= OC // 2 or mine[j] in ext[1 - g]]
                for j in both:
                    for r in list(named[j]):
                        to = [t for t in range(OC // 2) if t not in both and r not in named[t]]
                        named[j].remove(r); named[rng.choice(to)].add(r)
            elif not (plain or fixed or short):
                for j in range(OC // 2, UN):
                    for r in list(rng.permutation(list(named[j])))[:rng.integers(0, 3)]:
                        to = [t for t in range(OC // 2) if r not in named[t]]
                        named[j].remove(r); named[rng.choice(to)].add(r)
            at = rng.permutation(UN)
            for j, s in enumerate(named):
                if s: union[d, g, at[j]] = mine[j]
                for r in s: own[r][d].append((mine[j], at[j]))
    send, place, un = [], np.full((N, N, CAPP), -1), []
    for r in range(N):
        send.append(table(rng.permutation(T))); u = []
        for d in range(N):
            o = [own[r][d][i] for i in rng.permutation(CAPP)]
            place[d, r] = [v for v, _ in o]; u += [w for _, w in o]
        un.append(table(u))
    return {"send": np.stack(send), "place": np.stack([table(place[d].reshape(-1)) for d in range(N)]), "un": np.stack(un), "upl": np.stack([padded(union[d].reshape(-1), 64) for d in range(N)])}
def setup_inputs(rng):
    return {"a": f(rng, N, 128, 4 * 512), "b": f(rng, N, 128, 4 * T), **lists(rng)}
def setup_inputs_blocks(rng):
    return {**setup_inputs(rng), **lists(rng, blocks=True, plain=True)}
def setup_inputs_lossless(rng):
    d = setup_inputs(rng)
    a = np.zeros((N, 128, 4 * 128, 4), np.float32)
    for r in range(N):
        k = rng.integers(0, 512, size=4 * 128)
        a[r, k // 4, np.arange(4 * 128), k % 4] = 1.0
    size = 2.0 ** rng.integers(-4, 5, size=(N, OC)); b = rng.integers(-1, 2, size=(N, 128, T, 4)).astype(np.float64)
    for r in range(N):
        s = entries(d["send"][r]).reshape(N, CAPP)
        for o in range(N): b[r][:, s[o]] *= size[o][entries(d["place"][o]).reshape(N, CAPP)[r]][None, :, None]
    d["a"], d["b"] = a.reshape(N, 128, 4 * 512).astype(BF), b.reshape(N, 128, 4 * T).astype(np.float32).astype(BF)
    return d
def setup_inputs_pairs(rng):
    return {**setup_inputs(rng), **lists(rng, fixed=True)}
def setup_inputs_short(rng):
    return {**setup_inputs(rng), **lists(rng, short=True)}
def setup_inputs_spread(rng):
    d = setup_inputs(rng); d["b"] = wide(rng, N, 128, 4 * T); return d
def check_inputs(x):
    b = []
    seen = np.zeros((N, OC), int)
    for r in range(N):
        s, u = entries(x["send"][r]), entries(x["un"][r]).reshape(N, CAPP)
        if sorted(s.tolist()) != list(range(T)): b.append("send")
        if u.min() < 0 or u.max() >= UN: b.append("un")
        for o in range(N):
            p = entries(x["place"][o]).reshape(N, CAPP)[r]
            if p.min() < 0 or p.max() >= OC or len(set(p.tolist())) != CAPP: b.append("place")
            w = entries(x["upl"][o])[:2 * UN].reshape(2, UN)[HOST[r]]
            if (w[u[o]] != p).any(): b.append("upl")
            seen[o][p] += 1
    for o in range(N):
        for g in range(2):
            w = entries(x["upl"][o]); bad = w.min() < -1 or w.max() >= OC or (w[2 * UN:] != -1).any(); w = w[:2 * UN].reshape(2, UN)[g]; w = w[w >= 0]
            if len(set(w.tolist())) != len(w): b.append("upl twice")
    if seen.min() < 2: b.append("a column with fewer than two terms")
    return b
def reference(a, b, send, place, un, upl):
    Z = [term(a[r], mx_ref.quantize(b[r])).reshape(128, T, 4) for r in range(N)]
    y = np.zeros((N, 128, 4 * OC), np.float32)
    for o in range(N):
        parts = []
        for r in range(N):
            t = np.zeros((128, OC, 4), np.float32); t[:, entries(place[o]).reshape(N, CAPP)[r]] = Z[r][:, entries(send[r]).reshape(N, CAPP)[o]]
            parts.append(t.reshape(128, 4 * OC))
        y[o] = mx_ref.total(parts)
    return {"y": y}

@@ -1,0 +1,314 @@
+from concourse.bass import DstId, RemoteDMATransfer
+from concourse.mybir import dt, AluOpType, ActivationFunctionType
+
+UN, OC = 32, 56
+H = OC + UN
+SEC = 2 * UN + 128
+RX = 3 * SEC
+
+SCRATCH = {
+    "at": ("sbuf", [128, 2048], "bfloat16"),
+    "bt": ("sbuf", [128, 512], "bfloat16"),
+    "aq": ("sbuf", [128, 512], "float8_e4m3fn_x4"),
+    "asc": ("sbuf", [128, 512], "uint8"),
+    "bw": ("sbuf", [128, 1024], "bfloat16"),
+    "bq": ("sbuf", [128, 256], "float8_e4m3fn_x4"),
+    "bsc": ("sbuf", [128, 256], "uint8"),
+    "dn": ("sbuf", [128, 512], "bfloat16"),
+    "dg": ("sbuf", [128, 520], "bfloat16"),
+    "dg1": ("sbuf", [128, 520], "bfloat16"),
+    "ex": ("sbuf", [128, RX + 160], "float8_e4m3fn_x4"),
+    "exs": ("sbuf", [128, RX + 160], "uint8"),
+    "zt": ("sbuf", [128, 1024], "bfloat16"),
+    "zq": ("sbuf", [128, 256], "float8_e4m3fn_x4"),
+    "zs": ("sbuf", [128, 256], "uint8"),
+    "ct": ("sbuf", [128, 512], "bfloat16"),
+    "cq": ("sbuf", [128, 128], "float8_e4m3fn_x4"),
+    "cs": ("sbuf", [128, 128], "uint8"),
+    "li": ("sbuf", [128, 16], "int32"),
+    "xu": ("sbuf", [128, 8], "int32"),
+    "base": ("sbuf", [128, 8], "int32"),
+    "so": ("sbuf", [128, 32], "uint16"),
+    "uo": ("sbuf", [128, 32], "uint16"),
+    "up": ("sbuf", [128, 4], "int32"),
+    "pidx": ("sbuf", [128, 4], "int32"),
+    "pm": ("sbuf", [128, 4], "int32"),
+    "kc": ("sbuf", [128, 4], "int32"),
+    "rb": ("sbuf", [128, 4], "int32"),
+    "neg": ("sbuf", [128, 4], "int32"),
+    "po": ("sbuf", [128, 4], "uint16"),
+    "q4": ("sbuf", [128, 4], "int32"),
+    "q4f": ("sbuf", [128, 4], "float32"),
+    "p3": ("sbuf", [128, 4], "int32"),
+    "p3f": ("sbuf", [128, 4], "float32"),
+    "sv": ("sbuf", [128, 2 * UN], "float32"),
+    "uc": ("sbuf", [128, 2 * H], "float32"),
+    "ix": ("sbuf", [128, 2 * H], "float32"),
+    "i2": ("sbuf", [128, H], "float32"),
+    "i3": ("sbuf", [128, H // 2], "float32"),
+    "fo": ("sbuf", [128, H // 2], "uint16"),
+    "wl": ("sbuf", [128, 136], "float32"),
+    "wr": ("sbuf", [128, 136], "float32"),
+    "gl": ("sbuf", [128, 224], "float32"),
+    "yt": ("sbuf", [128, 224], "float32"),
+    "ps": ("psum", [128, 4096], "float32"),
+}
+SEMAPHORES = ["v", "s", "t", "gp", "ldl", "ldb", "lda0", "lda1", "ldu", "st", "ls",
+              "rc0", "rc1", "rc2", "rl0", "rl1", "rl2", "rr"]
+
+ADD, MUL, AND, SHR, LT, EQ = (AluOpType.add, AluOpType.mult, AluOpType.bitwise_and, AluOpType.arith_shift_right,
+                              AluOpType.is_lt, AluOpType.is_equal)
+COPY = ActivationFunctionType.Copy
+
+
+def mask_of(engines):
+    m = 0
+    for e in engines:
+        m |= 1 << e
+    return m
+
+
+def rank_program(g, core, T, topo):
+    rank = T.rank_of(core)
+    if rank is None:
+        return
+    V, S, PE, SY = g.vector, g.scalar, g.tensor, g.sync
+    sem = T.sem
+    mine = [c for c in T.cores if topo.host(c) == topo.host(core)]
+    other = [c for c in T.cores if topo.host(c) != topo.host(core)]
+    kr = mine.index(core)
+    hm = T.rank_of(mine[0])
+    ho = T.rank_of(other[0])
+    gm = 0 if topo.host(core) == topo.host(T.cores[0]) else 1
+    go = 1 - gm
+
+    tick = {"v": 0, "s": 0, "t": 0, "gp": 0}
+    seen = {}
+
+    def did(name, ins):
+        ins.then_inc(sem[name], 1)
+        tick[name] += 1
+        return (name, tick[name])
+
+    def need(qn, *ticks):
+        q = {"v": V, "s": S, "t": PE, "g": g, "y": SY}[qn]
+        for name, n in ticks:
+            if seen.get((qn, name), 0) < n:
+                seen[(qn, name)] = n
+                q.wait_ge(sem[name], n)
+
+    S.dma_start(T.bt[:], T.b[:]).then_inc(sem.ldb, 16)
+    for r in (0, 16):
+        SY.dma_start(T.li[r:r + 16, 0:8], T.send[:]).then_inc(sem.ldl, 16)
+    for r in (0, 16):
+        SY.dma_start(T.li[r:r + 16, 8:16], T.un[:]).then_inc(sem.ldl, 16)
+    S.dma_start(T.at[:, 0:1024], T.a[:, 0:1024]).then_inc(sem.lda0, 16)
+    SY.dma_start(T.at[:, 1024:2048], T.a[:, 1024:2048]).then_inc(sem.lda1, 16)
+    for r in (0, 16):
+        SY.dma_start(T.up[r:r + 16, :], T.upl[:]).then_inc(sem.ldu, 16)
+    LDL, LDB, LDU = ("ldl", 64), ("ldb", 16), ("ldu", 32)
+
+    ones = did("v", V.memset(T.dg1[:], 1.0))
+    if hm < ho:
+        b_base = did("gp", g.iota(T.base[:], [[UN, 4], [UN, 2]], -UN * kr - UN, 0))
+    else:
+        b_base = did("gp", g.iota(T.base[:], [[UN, 4], [-UN, 2]], -UN * kr, 0))
+    did("gp", g.iota(T.pidx[:], [[0, 4]], 0, 1))
+    need("g", ones)
+    diag = did("gp", g.affine_select(T.dg[:], T.dg1[:], [[-1, 520]], EQ, 0.0, 3, 4))
+    did("gp", g.iota(T.kc[:], [[0, 2], [16, 2]], OC + 1, 0))
+    did("gp", g.iota(T.rb[:], [[H, 2], [0, 2]], 0, 0))
+    did("gp", g.iota(T.sv[:], [[0, 2], [1, UN]], 0, 0, allow_small_or_imprecise_dtypes=True))
+    c_all = did("gp", g.iota(T.uc[:], [[0, H // 2], [1, 4]], 0, 0, allow_small_or_imprecise_dtypes=True))
+
+    did("v", V.memset(T.bw[:], 0.0))
+    did("v", V.memset(T.zt[:, 384:512], 0.0))
+    did("v", V.memset(T.zt[:, 896:1024], 0.0))
+    did("v", V.memset(T.ct[:, 128:512], 0.0))
+    did("v", V.memset(T.wl[:, 128:136], 0.0))
+    did("v", V.memset(T.wr[:, 128:136], 0.0))
+    z_all = did("v", V.memset(T.ix[:], float(UN)))
+    need("v", b_base)
+    base = did("v", V.tensor_scalar(T.base[:], T.base[:], 127, None, op0=AND))
+
+    def E(b):
+        o = SEC * b + UN
+        return T.ex[:, o:o + 128], T.exs[:, o:o + 128]
+
+    need("v", diag)
+    e_all = None
+    for b in range(4):
+        c, s = E(b)
+        e_all = did("v", V.quantize_mx(c, s, T.dg[:, 3 - b:3 - b + 512]))
+
+    need("v", LDL)
+    need("v", did("v", V.tensor_copy(T.li[32:64, :], T.li[0:32, :])))
+    need("v", did("v", V.tensor_copy(T.li[64:128, :], T.li[0:64, :])))
+
+    def offsets(out, src, h, at):
+        n = None
+        for t in range(4):
+            n = did("v", V.tensor_scalar(out[:, at + 4 * t:at + 4 * t + 4], src[:, h:8:2], 4, t, op0=MUL, op1=ADD))
+        return n
+
+    so_c = offsets(T.so, T.li, ho, 0)
+    need("s", LDB, so_c)
+    dn_c = did("s", S.activation(T.dn[:, 0:128], T.bt[:, 0:512].indirect(T.so[:, 0:8]), COPY))
+    need("v", LDB, so_c)
+    did("v", V.tensor_copy(T.dn[:, 128:256], T.bt[:, 0:512].indirect(T.so[:, 8:16])))
+    need("v", base, did("v", V.tensor_tensor(T.xu[:], T.li[:, 8:16], T.base[:], ADD)))
+    need("v", offsets(T.uo, T.xu, ho, 0), dn_c)
+    need("v", did("v", V.tensor_copy(T.bw[:, 0:512].indirect(T.uo[:, 0:16]), T.dn[:, 0:256])))
+    b_c = did("v", V.quantize_mx(T.bq[:, 0:128], T.bsc[:, 0:128], T.bw[:, 0:512]))
+    so_l = offsets(T.so, T.li, hm, 16)
+    uo_l = offsets(T.uo, T.xu, hm, 16)
+
+    a_q = []
+    for i in range(4):
+        need("v", ("lda%d" % (i // 2), 16))
+        a_q.append(did("v", V.quantize_mx(T.aq[:, 128 * i:128 * i + 128], T.asc[:, 128 * i:128 * i + 128],
+                                          T.at[:, 512 * i:512 * i + 512])))
+
+    bank_open = [False] * 8
+
+    def own(i, half, bank, stop):
+        need("t", a_q[i], b_c)
+        return did("t", PE.matmul_mx(T.ps[:, 512 * bank:512 * bank + 128],
+                                     T.aq[:, 128 * i:128 * i + 128], T.asc[:, 128 * i:128 * i + 128],
+                                     T.bq[:, 128 * half:128 * half + 128], T.bsc[:, 128 * half:128 * half + 128],
+                                     True, stop))
+
+    def unpack(b, col, bank, stop):
+        c, s = E(b)
+        need("t", e_all)
+        return did("t", PE.matmul_mx(T.ps[:, 512 * bank:512 * bank + 128], c, s,
+                                     T.ex[:, col:col + 128], T.exs[:, col:col + 128], not bank_open[bank], stop))
+
+    def copy(qn, out, in_, *ticks):
+        need(qn, *ticks)
+        return did(qn, S.activation(out, in_, COPY) if qn == "s" else V.tensor_copy(out, in_))
+
+    def ps(bank, lo, hi):
+        return T.ps[:, 512 * bank + lo:512 * bank + hi]
+
+    zc = [own(i, 0, i, True) for i in range(4)]
+    for i in range(4):
+        own(i, 0, 4 + i, False)
+        bank_open[4 + i] = True
+    cp = [copy("sssv"[i], T.zt[:, i:384:4], ps(i, UN, 128), zc[i]) for i in range(4)]
+    need("v", *cp)
+    zq_c = did("v", V.quantize_mx(T.zq[:, 0:128], T.zs[:, 0:128], T.zt[:, 0:512]))
+
+    peers = [mine[(kr + 1 + j) % 4] for j in range(3)]
+    sent = [0]
+
+    def cuts(en):
+        n = len(en)
+        return ([en[0:n // 4], en[n // 4:n // 2], en[n // 2:n]], [en[n // 2:3 * n // 4], en[3 * n // 4:n], en[0:n // 2]])
+
+    def hop1(kind, col, at):
+        for codes in (True, False):
+            tr = []
+            for j in range(3):
+                o = SEC * (2 - j) + at
+                a0 = col + UN * j
+                en = cuts(topo.engines(core, peers[j]))[0 if codes else 1][j]
+                if codes:
+                    src, dst = T.zq[:, a0:a0 + UN].bitcast(dt.uint8), T.ex[:, o:o + UN].bitcast(dt.uint8)
+                else:
+                    src, dst = T.zs[:, a0:a0 + UN], T.exs[:, o:o + UN]
+                rid, pid = topo.addr(peers[j], core)
+                tr.append(RemoteDMATransfer(dst_ids=[DstId(rid=rid, pnc=pid)], dma_engine_mask=mask_of(en),
+                                            remote_sem=sem["%s%d" % (kind, 2 - j)], src=src, dst=dst))
+                sent[0] += len(en)
+            g.remote_dma_fused(tr, local_sem=sem.ls)
+
+    def got(s):
+        c = cuts(topo.engines(mine[(kr + 1 + s) % 4], core))
+        return len(c[0][2 - s]) + len(c[1][2 - s])
+
+    need("g", zq_c)
+    hop1("rc", 0, 0)
+
+    need("s", so_l)
+    dn_l = did("s", S.activation(T.dn[:, 256:512], T.bt[:, 0:512].indirect(T.so[:, 16:32]), COPY))
+    need("v", uo_l, dn_l)
+    need("v", did("v", V.tensor_copy(T.bw[:, 512:1024].indirect(T.uo[:, 16:32]), T.dn[:, 256:512])))
+    b_l = did("v", V.quantize_mx(T.bq[:, 128:256], T.bsc[:, 128:256], T.bw[:, 512:1024]))
+    need("t", b_l)
+    zl = []
+    for i in range(4):
+        need("t", cp[i])
+        zl.append(own(i, 1, i, True))
+    lp = [copy("svsv"[i], T.zt[:, 512 + i:896:4], ps(i, 0, 96), zl[i]) for i in range(4)]
+    need("v", *lp)
+    zq_l = did("v", V.quantize_mx(T.zq[:, 128:256], T.zs[:, 128:256], T.zt[:, 512:1024]))
+    need("g", zq_l)
+    hop1("rl", 128, UN + 128)
+
+    last = [None] * 4
+    for s in range(3):
+        need("t", ("rc%d" % s, got(s)))
+        for b in range(4):
+            last[b] = unpack(b, SEC * s, 4 + b, s == 2)
+    cc = [copy("svsv"[b], T.ct[:, b:128:4], ps(4 + b, 0, UN), last[b]) for b in range(4)]
+    need("v", *cc)
+    c_q = did("v", V.quantize_mx(T.cq[:], T.cs[:], T.ct[:]))
+
+    far = other[kr]
+    rid, pid = topo.addr(far, core)
+    m = topo.mask(core, far)
+    need("g", c_q)
+    g.remote_dma(T.ex[:, RX:RX + UN].bitcast(dt.uint8), T.cq[:, 0:UN].bitcast(dt.uint8), sem.rr, sem.ls, pid, rid, m)
+    g.remote_dma(T.exs[:, RX:RX + UN], T.cs[:, 0:UN], sem.rr, sem.ls, pid, rid, m)
+    sent[0] += 2 * len(topo.engines(core, far))
+
+    for i in range(4):
+        need("t", lp[i])
+        own(i, 1, i, False)
+        bank_open[i] = True
+    for s in range(3):
+        need("t", ("rl%d" % s, got(s)))
+        for b in range(4):
+            last[b] = unpack(b, SEC * s + 2 * UN, b, s == 2)
+    wl = [copy("s", T.wl[:, b:128:4], ps(b, 96, 128), last[b]) for b in range(4)]
+
+    need("v", LDU, c_all)
+    need("v", did("v", V.tensor_copy(T.up[32:64, :], T.up[0:32, :])))
+    did("v", V.tensor_copy(T.up[64:128, :], T.up[0:64, :]))
+    did("v", V.tensor_scalar(T.pm[:], T.pidx[:], 15, None, op0=AND))
+    did("v", V.tensor_scalar(T.q4[:], T.pidx[:], 15, 2, op0=AND, op1=SHR))
+    need("v", did("v", V.tensor_scalar(T.p3[:], T.pidx[:], 3, None, op0=AND)))
+    did("v", V.tensor_copy(T.q4f[:], T.q4[:]))
+    did("v", V.tensor_copy(T.p3f[:], T.p3[:]))
+    did("v", V.tensor_scalar(T.neg[:], T.up[:], 0, None, op0=LT))
+    did("v", V.tensor_tensor(T.kc[:], T.kc[:], T.pm[:], ADD))
+    need("v", did("v", V.tensor_tensor(T.rb[:], T.rb[:], T.up[:], ADD)))
+    x = did("v", V.tensor_tensor(T.neg[:], T.neg[:], T.kc[:], MUL))
+    did("v", V.tensor_scalar(T.uc[:], T.uc[:], T.q4f[:, 0:1], None, op0=EQ))
+    need("v", x)
+    need("v", did("v", V.tensor_tensor(T.rb[:], T.rb[:], T.neg[:], ADD)))
+    need("v", did("v", V.tensor_copy(T.po[:], T.rb[:])))
+    need("v", did("v", V.tensor_copy(T.ix[:, 0:2 * H].indirect(T.po[:, 0:4]), T.sv[:])))
+    need("v", did("v", V.tensor_tensor(T.ix[:], T.ix[:], T.uc[:], MUL)))
+    need("v", did("v", V.tensor_tensor(T.i2[:], T.ix[:, 0:2 * H:2], T.ix[:, 1:2 * H:2], ADD)))
+    need("v", did("v", V.tensor_tensor(T.i3[:], T.i2[:, 0:H:2], T.i2[:, 1:H:2], ADD)))
+    fo = did("v", V.tensor_scalar(T.fo[:], T.i3[:], 4.0, T.p3f[:, 0:1], op0=MUL, op1=ADD))
+    need("s", fo, z_all, *wl)
+    q = H // 4
+    gl = did("s", S.activation(T.gl[:], T.wl[:, 0:136].indirect(T.fo[:, q * gm:q * gm + OC // 4]), COPY))
+
+    need("t", ("rr", 2 * len(topo.engines(far, core))))
+    rc = []
+    for b in range(4):
+        bank_open[4 + b] = False
+        need("t", cc[b])
+        rc.append(unpack(b, RX, 4 + b, True))
+    wr = [copy("svsv"[b], T.wr[:, b:128:4], ps(4 + b, 0, UN), rc[b]) for b in range(4)]
+    need("v", fo, gl, *wr)
+    y = did("v", V.tensor_tensor(T.yt[:], T.wr[:, 0:136].indirect(T.fo[:, q * go:q * go + OC // 4]), T.gl[:], ADD))
+    need("y", y)
+    SY.dma_start(T.y[:], T.yt[:]).then_inc(sem.st, 16)
+    SY.wait_ge(sem.st, 16)
+    g.wait_ge(sem.ls, sent[0])
+    need("g", ("v", tick["v"]), ("s", tick["s"]), ("t", tick["t"]))

@@ -15,8 +15,9 @@ SCRATCH = {
     "bq": ("sbuf", [128, 256], "float8_e4m3fn_x4"),
     "bsc": ("sbuf", [128, 256], "uint8"),
     "dn": ("sbuf", [128, 512], "bfloat16"),
-    "dg": ("sbuf", [128, 520], "bfloat16"),
-    "dg1": ("sbuf", [128, 520], "bfloat16"),
+    "dg": ("sbuf", [128, 516], "bfloat16"),
+    "one": ("sbuf", [128, 128], "bfloat16"),
+    "zb": ("sbuf", [128, 512], "bfloat16"),
     "ex": ("sbuf", [128, RX + 160], "float8_e4m3fn_x4"),
     "exs": ("sbuf", [128, RX + 160], "uint8"),
     "zt": ("sbuf", [128, 1024], "bfloat16"),
@@ -97,37 +98,44 @@ def rank_program(g, core, T, topo):
                 seen[(qn, name)] = n
                 q.wait_ge(sem[name], n)
 
-    S.dma_start(T.bt[:], T.b[:]).then_inc(sem.ldb, 16)
+    def copy(qn, out, in_, *ticks):
+        need(qn, *ticks)
+        return did(qn, S.activation(out, in_, COPY) if qn == "s" else V.tensor_copy(out, in_))
+
+    def iota(out, pattern, base, cm=0, fl=False):
+        return did("gp", g.iota(out, pattern, base, cm, allow_small_or_imprecise_dtypes=True) if fl
+                   else g.iota(out, pattern, base, cm))
+
     for r in (0, 16):
         SY.dma_start(T.li[r:r + 16, 0:8], T.send[:]).then_inc(sem.ldl, 16)
-    for r in (0, 16):
-        SY.dma_start(T.li[r:r + 16, 8:16], T.un[:]).then_inc(sem.ldl, 16)
-    S.dma_start(T.at[:, 0:1024], T.a[:, 0:1024]).then_inc(sem.lda0, 16)
-    SY.dma_start(T.at[:, 1024:2048], T.a[:, 1024:2048]).then_inc(sem.lda1, 16)
+        S.dma_start(T.li[r:r + 16, 8:16], T.un[:]).then_inc(sem.ldl, 16)
+    S.dma_start(T.bt[:], T.b[:]).then_inc(sem.ldb, 16)
+    SY.dma_start(T.at[:, 0:1024], T.a[:, 0:1024]).then_inc(sem.lda0, 16)
+    S.dma_start(T.at[:, 1024:2048], T.a[:, 1024:2048]).then_inc(sem.lda1, 16)
     for r in (0, 16):
         SY.dma_start(T.up[r:r + 16, :], T.upl[:]).then_inc(sem.ldu, 16)
     LDL, LDB, LDU = ("ldl", 64), ("ldb", 16), ("ldu", 32)
 
-    ones = did("v", V.memset(T.dg1[:], 1.0))
-    if hm < ho:
-        b_base = did("gp", g.iota(T.base[:], [[UN, 4], [UN, 2]], -UN * kr - UN, 0))
-    else:
-        b_base = did("gp", g.iota(T.base[:], [[UN, 4], [-UN, 2]], -UN * kr, 0))
-    did("gp", g.iota(T.pidx[:], [[0, 4]], 0, 1))
-    need("g", ones)
-    diag = did("gp", g.affine_select(T.dg[:], T.dg1[:], [[-1, 520]], EQ, 0.0, 3, 4))
-    did("gp", g.iota(T.kc[:], [[0, 2], [16, 2]], OC + 1, 0))
-    did("gp", g.iota(T.rb[:], [[H, 2], [0, 2]], 0, 0))
-    did("gp", g.iota(T.sv[:], [[0, 2], [1, UN]], 0, 0, allow_small_or_imprecise_dtypes=True))
-    c_all = did("gp", g.iota(T.uc[:], [[0, H // 2], [1, 4]], 0, 0, allow_small_or_imprecise_dtypes=True))
-
-    did("v", V.memset(T.bw[:], 0.0))
+    did("v", V.memset(T.one[:], 1.0))
+    z_dg = did("v", V.memset(T.dg[:], 0.0))
+    z_zb = did("v", V.memset(T.zb[:], 0.0))
+    did("v", V.memset(T.bw[:, 0:512], 0.0))
     did("v", V.memset(T.zt[:, 384:512], 0.0))
-    did("v", V.memset(T.zt[:, 896:1024], 0.0))
-    did("v", V.memset(T.ct[:, 128:512], 0.0))
-    did("v", V.memset(T.wl[:, 128:136], 0.0))
-    did("v", V.memset(T.wr[:, 128:136], 0.0))
-    z_all = did("v", V.memset(T.ix[:], float(UN)))
+    b_base = iota(T.base[:], [[UN, 4], [UN, 2]] if hm < ho else [[UN, 4], [-UN, 2]], -UN * kr - (UN if hm < ho else 0))
+    need("g", z_dg)
+    diag = did("gp", g.affine_select(T.dg[:, 3:515:4], T.one[:], [[-1, 128]], EQ, 0.0, 0, 1))
+    iota(T.pidx[:], [[0, 4]], 0, 1)
+    iota(T.kc[:], [[0, 2], [16, 2]], OC + 1)
+    iota(T.rb[:], [[H, 2], [0, 2]], 0)
+    iota(T.sv[:], [[0, 2], [1, UN]], 0, 0, True)
+    iota(T.uc[:], [[0, H // 2], [1, 4]], 0, 0, True)
+    iota(T.ix[:], [[0, 2 * H]], UN, 0, True)
+    iota(T.wl[:, 128:136], [[0, 8]], 0, 0, True)
+    c_all = iota(T.wr[:, 128:136], [[0, 8]], 0, 0, True)
+    copy("s", T.bw[:, 512:1024], T.zb[:], z_zb)
+    copy("s", T.ct[:, 128:512], T.zb[:, 0:384])
+    copy("s", T.zt[:, 896:1024], T.zb[:, 0:128])
+
     need("v", b_base)
     base = did("v", V.tensor_scalar(T.base[:], T.base[:], 127, None, op0=AND))
 
@@ -142,26 +150,19 @@ def rank_program(g, core, T, topo):
         e_all = did("v", V.quantize_mx(c, s, T.dg[:, 3 - b:3 - b + 512]))
 
     need("v", LDL)
-    need("v", did("v", V.tensor_copy(T.li[32:64, :], T.li[0:32, :])))
-    need("v", did("v", V.tensor_copy(T.li[64:128, :], T.li[0:64, :])))
+    need("v", copy("v", T.li[32:64, :], T.li[0:32, :]))
+    need("v", copy("v", T.li[64:128, :], T.li[0:64, :]))
 
     def offsets(out, src, h, at):
-        n = None
-        for t in range(4):
-            n = did("v", V.tensor_scalar(out[:, at + 4 * t:at + 4 * t + 4], src[:, h:8:2], 4, t, op0=MUL, op1=ADD))
-        return n
+        return [did("v", V.tensor_scalar(out[:, at + 4 * t:at + 4 * t + 4], src[:, h:8:2], 4, t, op0=MUL, op1=ADD))
+                for t in range(4)]
 
     so_c = offsets(T.so, T.li, ho, 0)
-    need("s", LDB, so_c)
-    dn_c = did("s", S.activation(T.dn[:, 0:128], T.bt[:, 0:512].indirect(T.so[:, 0:8]), COPY))
-    need("v", LDB, so_c)
-    did("v", V.tensor_copy(T.dn[:, 128:256], T.bt[:, 0:512].indirect(T.so[:, 8:16])))
+    copy("s", T.dn[:, 0:128], T.bt[:, 0:512].indirect(T.so[:, 0:8]), LDB, so_c[1])
+    dn_c = copy("s", T.dn[:, 128:256], T.bt[:, 0:512].indirect(T.so[:, 8:16]), so_c[3])
     need("v", base, did("v", V.tensor_tensor(T.xu[:], T.li[:, 8:16], T.base[:], ADD)))
-    need("v", offsets(T.uo, T.xu, ho, 0), dn_c)
-    need("v", did("v", V.tensor_copy(T.bw[:, 0:512].indirect(T.uo[:, 0:16]), T.dn[:, 0:256])))
+    need("v", copy("v", T.bw[:, 0:512].indirect(T.uo[:, 0:16]), T.dn[:, 0:256], offsets(T.uo, T.xu, ho, 0)[3], dn_c))
     b_c = did("v", V.quantize_mx(T.bq[:, 0:128], T.bsc[:, 0:128], T.bw[:, 0:512]))
-    so_l = offsets(T.so, T.li, hm, 16)
-    uo_l = offsets(T.uo, T.xu, hm, 16)
 
     a_q = []
     for i in range(4):
@@ -184,10 +185,6 @@ def rank_program(g, core, T, topo):
         return did("t", PE.matmul_mx(T.ps[:, 512 * bank:512 * bank + 128], c, s,
                                      T.ex[:, col:col + 128], T.exs[:, col:col + 128], not bank_open[bank], stop))
 
-    def copy(qn, out, in_, *ticks):
-        need(qn, *ticks)
-        return did(qn, S.activation(out, in_, COPY) if qn == "s" else V.tensor_copy(out, in_))
-
     def ps(bank, lo, hi):
         return T.ps[:, 512 * bank + lo:512 * bank + hi]
 
@@ -206,34 +203,27 @@ def rank_program(g, core, T, topo):
         n = len(en)
         return ([en[0:n // 4], en[n // 4:n // 2], en[n // 2:n]], [en[n // 2:3 * n // 4], en[3 * n // 4:n], en[0:n // 2]])
 
-    def hop1(kind, col, at):
-        for codes in (True, False):
-            tr = []
-            for j in range(3):
-                o = SEC * (2 - j) + at
-                a0 = col + UN * j
-                en = cuts(topo.engines(core, peers[j]))[0 if codes else 1][j]
-                if codes:
-                    src, dst = T.zq[:, a0:a0 + UN].bitcast(dt.uint8), T.ex[:, o:o + UN].bitcast(dt.uint8)
-                else:
-                    src, dst = T.zs[:, a0:a0 + UN], T.exs[:, o:o + UN]
-                rid, pid = topo.addr(peers[j], core)
-                tr.append(RemoteDMATransfer(dst_ids=[DstId(rid=rid, pnc=pid)], dma_engine_mask=mask_of(en),
-                                            remote_sem=sem["%s%d" % (kind, 2 - j)], src=src, dst=dst))
-                sent[0] += len(en)
-            g.remote_dma_fused(tr, local_sem=sem.ls)
+    def sides(codes, col, o):
+        if codes:
+            return T.ex[:, o:o + UN].bitcast(dt.uint8), T.zq[:, col:col + UN].bitcast(dt.uint8)
+        return T.exs[:, o:o + UN], T.zs[:, col:col + UN]
 
     def got(s):
         c = cuts(topo.engines(mine[(kr + 1 + s) % 4], core))
         return len(c[0][2 - s]) + len(c[1][2 - s])
 
     need("g", zq_c)
-    hop1("rc", 0, 0)
+    for j in range(3):
+        rid, pid = topo.addr(peers[j], core)
+        for codes in (True, False):
+            dst, src = sides(codes, UN * j, SEC * (2 - j))
+            g.remote_dma(dst, src, sem["rc%d" % (2 - j)], sem.ls, pid, rid, topo.mask(core, peers[j]))
+            sent[0] += len(topo.engines(core, peers[j]))
 
-    need("s", so_l)
-    dn_l = did("s", S.activation(T.dn[:, 256:512], T.bt[:, 0:512].indirect(T.so[:, 16:32]), COPY))
-    need("v", uo_l, dn_l)
-    need("v", did("v", V.tensor_copy(T.bw[:, 512:1024].indirect(T.uo[:, 16:32]), T.dn[:, 256:512])))
+    so_l = offsets(T.so, T.li, hm, 16)[3]
+    dn_l = copy("s", T.dn[:, 256:512], T.bt[:, 0:512].indirect(T.so[:, 16:32]), so_l)
+    uo_l = offsets(T.uo, T.xu, hm, 16)[3]
+    need("v", copy("v", T.bw[:, 512:1024].indirect(T.uo[:, 16:32]), T.dn[:, 256:512], uo_l, dn_l))
     b_l = did("v", V.quantize_mx(T.bq[:, 128:256], T.bsc[:, 128:256], T.bw[:, 512:1024]))
     need("t", b_l)
     zl = []
@@ -244,13 +234,22 @@ def rank_program(g, core, T, topo):
     need("v", *lp)
     zq_l = did("v", V.quantize_mx(T.zq[:, 128:256], T.zs[:, 128:256], T.zt[:, 512:1024]))
     need("g", zq_l)
-    hop1("rl", 128, UN + 128)
+    for codes in (True, False):
+        tr = []
+        for j in range(3):
+            dst, src = sides(codes, 128 + UN * j, SEC * (2 - j) + UN + 128)
+            en = cuts(topo.engines(core, peers[j]))[0 if codes else 1][j]
+            rid, pid = topo.addr(peers[j], core)
+            tr.append(RemoteDMATransfer(dst_ids=[DstId(rid=rid, pnc=pid)], dma_engine_mask=mask_of(en),
+                                        remote_sem=sem["rl%d" % (2 - j)], src=src, dst=dst))
+            sent[0] += len(en)
+        g.remote_dma_fused(tr, local_sem=sem.ls)
 
     last = [None] * 4
-    for s in range(3):
-        need("t", ("rc%d" % s, got(s)))
+    for s in (2, 1, 0):
+        need("t", ("rc%d" % s, 2 * len(topo.engines(mine[(kr + 1 + s) % 4], core))))
         for b in range(4):
-            last[b] = unpack(b, SEC * s, 4 + b, s == 2)
+            last[b] = unpack(b, SEC * s, 4 + b, s == 0)
     cc = [copy("svsv"[b], T.ct[:, b:128:4], ps(4 + b, 0, UN), last[b]) for b in range(4)]
     need("v", *cc)
     c_q = did("v", V.quantize_mx(T.cq[:], T.cs[:], T.ct[:]))
@@ -274,13 +273,13 @@ def rank_program(g, core, T, topo):
     wl = [copy("s", T.wl[:, b:128:4], ps(b, 96, 128), last[b]) for b in range(4)]
 
     need("v", LDU, c_all)
-    need("v", did("v", V.tensor_copy(T.up[32:64, :], T.up[0:32, :])))
-    did("v", V.tensor_copy(T.up[64:128, :], T.up[0:64, :]))
+    need("v", copy("v", T.up[32:64, :], T.up[0:32, :]))
+    copy("v", T.up[64:128, :], T.up[0:64, :])
     did("v", V.tensor_scalar(T.pm[:], T.pidx[:], 15, None, op0=AND))
     did("v", V.tensor_scalar(T.q4[:], T.pidx[:], 15, 2, op0=AND, op1=SHR))
     need("v", did("v", V.tensor_scalar(T.p3[:], T.pidx[:], 3, None, op0=AND)))
-    did("v", V.tensor_copy(T.q4f[:], T.q4[:]))
-    did("v", V.tensor_copy(T.p3f[:], T.p3[:]))
+    copy("v", T.q4f[:], T.q4[:])
+    copy("v", T.p3f[:], T.p3[:])
     did("v", V.tensor_scalar(T.neg[:], T.up[:], 0, None, op0=LT))
     did("v", V.tensor_tensor(T.kc[:], T.kc[:], T.pm[:], ADD))
     need("v", did("v", V.tensor_tensor(T.rb[:], T.rb[:], T.up[:], ADD)))
@@ -288,15 +287,14 @@ def rank_program(g, core, T, topo):
     did("v", V.tensor_scalar(T.uc[:], T.uc[:], T.q4f[:, 0:1], None, op0=EQ))
     need("v", x)
     need("v", did("v", V.tensor_tensor(T.rb[:], T.rb[:], T.neg[:], ADD)))
-    need("v", did("v", V.tensor_copy(T.po[:], T.rb[:])))
-    need("v", did("v", V.tensor_copy(T.ix[:, 0:2 * H].indirect(T.po[:, 0:4]), T.sv[:])))
+    need("v", copy("v", T.po[:], T.rb[:]))
+    need("v", copy("v", T.ix[:, 0:2 * H].indirect(T.po[:, 0:4]), T.sv[:]))
     need("v", did("v", V.tensor_tensor(T.ix[:], T.ix[:], T.uc[:], MUL)))
     need("v", did("v", V.tensor_tensor(T.i2[:], T.ix[:, 0:2 * H:2], T.ix[:, 1:2 * H:2], ADD)))
     need("v", did("v", V.tensor_tensor(T.i3[:], T.i2[:, 0:H:2], T.i2[:, 1:H:2], ADD)))
     fo = did("v", V.tensor_scalar(T.fo[:], T.i3[:], 4.0, T.p3f[:, 0:1], op0=MUL, op1=ADD))
-    need("s", fo, z_all, *wl)
     q = H // 4
-    gl = did("s", S.activation(T.gl[:], T.wl[:, 0:136].indirect(T.fo[:, q * gm:q * gm + OC // 4]), COPY))
+    gl = copy("s", T.gl[:], T.wl[:, 0:136].indirect(T.fo[:, q * gm:q * gm + OC // 4]), fo, c_all, *wl)
 
     need("t", ("rr", 2 * len(topo.engines(far, core))))
     rc = []

@@ -17,7 +17,6 @@ SCRATCH = {
     "dn": ("sbuf", [128, 512], "bfloat16"),
     "dg": ("sbuf", [128, 516], "bfloat16"),
     "one": ("sbuf", [128, 128], "bfloat16"),
-    "zb": ("sbuf", [128, 512], "bfloat16"),
     "ex": ("sbuf", [128, RX + 160], "float8_e4m3fn_x4"),
     "exs": ("sbuf", [128, RX + 160], "uint8"),
     "zt": ("sbuf", [128, 1024], "bfloat16"),
@@ -27,10 +26,10 @@ SCRATCH = {
     "cq": ("sbuf", [128, 128], "float8_e4m3fn_x4"),
     "cs": ("sbuf", [128, 128], "uint8"),
     "li": ("sbuf", [128, 16], "int32"),
-    "xu": ("sbuf", [128, 8], "int32"),
-    "base": ("sbuf", [128, 8], "int32"),
-    "so": ("sbuf", [128, 32], "uint16"),
-    "uo": ("sbuf", [128, 32], "uint16"),
+    "lx": ("sbuf", [128, 16], "int32"),
+    "base": ("sbuf", [128, 16], "int32"),
+    "oc": ("sbuf", [128, 32], "uint16"),
+    "ol": ("sbuf", [128, 32], "uint16"),
     "up": ("sbuf", [128, 4], "int32"),
     "pidx": ("sbuf", [128, 4], "int32"),
     "pm": ("sbuf", [128, 4], "int32"),
@@ -60,13 +59,6 @@ SEMAPHORES = ["v", "s", "t", "gp", "ldl", "ldb", "lda0", "lda1", "ldu", "st", "l
 ADD, MUL, AND, SHR, LT, EQ = (AluOpType.add, AluOpType.mult, AluOpType.bitwise_and, AluOpType.arith_shift_right,
                               AluOpType.is_lt, AluOpType.is_equal)
 COPY = ActivationFunctionType.Copy
-
-
-def mask_of(engines):
-    m = 0
-    for e in engines:
-        m |= 1 << e
-    return m
 
 
 def rank_program(g, core, T, topo):
@@ -106,71 +98,81 @@ def rank_program(g, core, T, topo):
         return did("gp", g.iota(out, pattern, base, cm, allow_small_or_imprecise_dtypes=True) if fl
                    else g.iota(out, pattern, base, cm))
 
+    def load_up(q, r):
+        q.dma_start(T.up[r:r + 16, :], T.upl[:]).then_inc(sem.ldu, 16)
+
     for r in (0, 16):
         SY.dma_start(T.li[r:r + 16, 0:8], T.send[:]).then_inc(sem.ldl, 16)
         S.dma_start(T.li[r:r + 16, 8:16], T.un[:]).then_inc(sem.ldl, 16)
     S.dma_start(T.bt[:], T.b[:]).then_inc(sem.ldb, 16)
-    SY.dma_start(T.at[:, 0:1024], T.a[:, 0:1024]).then_inc(sem.lda0, 16)
-    S.dma_start(T.at[:, 1024:2048], T.a[:, 1024:2048]).then_inc(sem.lda1, 16)
-    for r in (0, 16):
-        SY.dma_start(T.up[r:r + 16, :], T.upl[:]).then_inc(sem.ldu, 16)
-    LDL, LDB, LDU = ("ldl", 64), ("ldb", 16), ("ldu", 32)
+    load_up(SY, 0)
+    SY.dma_start(T.at[:, 0:1536], T.a[:, 0:1536]).then_inc(sem.lda0, 16)
+    load_up(S, 16)
+    S.dma_start(T.at[:, 1536:2048], T.a[:, 1536:2048]).then_inc(sem.lda1, 16)
+    need("y", ("lda1", 16))
+    for r in range(32, 128, 16):
+        load_up(SY, r)
+    LDL, LDB, LDU = ("ldl", 64), ("ldb", 16), ("ldu", 128)
 
+    z_bw = did("v", V.memset(T.bw[:, 0:512], 0.0))
     did("v", V.memset(T.one[:], 1.0))
     z_dg = did("v", V.memset(T.dg[:], 0.0))
-    z_zb = did("v", V.memset(T.zb[:], 0.0))
-    did("v", V.memset(T.bw[:, 0:512], 0.0))
     did("v", V.memset(T.zt[:, 384:512], 0.0))
-    b_base = iota(T.base[:], [[UN, 4], [UN, 2]] if hm < ho else [[UN, 4], [-UN, 2]], -UN * kr - (UN if hm < ho else 0))
-    need("g", z_dg)
-    diag = did("gp", g.affine_select(T.dg[:, 3:515:4], T.one[:], [[-1, 128]], EQ, 0.0, 0, 1))
+    did("v", V.memset(T.zt[:, 896:1024], 0.0))
+    b_base = iota(T.base[:, 8:16], [[UN, 4], [UN, 2]] if hm < ho else [[UN, 4], [-UN, 2]], -UN * kr - (UN if hm < ho else 0))
+    b_zero = iota(T.base[:, 0:8], [[0, 8]], 0)
     iota(T.pidx[:], [[0, 4]], 0, 1)
     iota(T.kc[:], [[0, 2], [16, 2]], OC + 1)
     iota(T.rb[:], [[H, 2], [0, 2]], 0)
+    need("g", z_dg)
+    diag = did("gp", g.affine_select(T.dg[:, 3:515:4], T.one[:], [[-1, 128]], EQ, 0.0, 0, 1))
     iota(T.sv[:], [[0, 2], [1, UN]], 0, 0, True)
     iota(T.uc[:], [[0, H // 2], [1, 4]], 0, 0, True)
     iota(T.ix[:], [[0, 2 * H]], UN, 0, True)
     iota(T.wl[:, 128:136], [[0, 8]], 0, 0, True)
     c_all = iota(T.wr[:, 128:136], [[0, 8]], 0, 0, True)
-    copy("s", T.bw[:, 512:1024], T.zb[:], z_zb)
-    copy("s", T.ct[:, 128:512], T.zb[:, 0:384])
-    copy("s", T.zt[:, 896:1024], T.zb[:, 0:128])
+    copy("s", T.bw[:, 512:1024], T.bw[:, 0:512], z_bw)
 
     need("v", b_base)
-    base = did("v", V.tensor_scalar(T.base[:], T.base[:], 127, None, op0=AND))
+    did("v", V.tensor_scalar(T.base[:, 8:16], T.base[:, 8:16], 127, None, op0=AND))
 
     def E(b):
         o = SEC * b + UN
         return T.ex[:, o:o + 128], T.exs[:, o:o + 128]
 
-    need("v", diag)
-    e_all = None
-    for b in range(4):
+    e_all = [None]
+
+    def make_e(b):
+        need("v", diag)
         c, s = E(b)
-        e_all = did("v", V.quantize_mx(c, s, T.dg[:, 3 - b:3 - b + 512]))
+        e_all[0] = did("v", V.quantize_mx(c, s, T.dg[:, 3 - b:3 - b + 512]))
 
-    need("v", LDL)
-    need("v", copy("v", T.li[32:64, :], T.li[0:32, :]))
-    need("v", copy("v", T.li[64:128, :], T.li[0:64, :]))
+    need("v", LDL, b_zero)
+    x = copy("v", T.li[32:64, :], T.li[0:32, :])
+    need("v", x)
+    for r in (0, 64):
+        x = did("v", V.tensor_tensor(T.lx[r:r + 64, :], T.li[0:64, :], T.base[0:64, :], ADD))
+    need("v", x)
 
-    def offsets(out, src, h, at):
-        return [did("v", V.tensor_scalar(out[:, at + 4 * t:at + 4 * t + 4], src[:, h:8:2], 4, t, op0=MUL, op1=ADD))
-                for t in range(4)]
+    def offsets(out, h, at, t, k):
+        return did("v", V.tensor_scalar(out[:, at:at + 7 * k + 1:k], T.lx[:, h:16:2], 4, t, op0=MUL, op1=ADD))
 
-    so_c = offsets(T.so, T.li, ho, 0)
-    copy("s", T.dn[:, 0:128], T.bt[:, 0:512].indirect(T.so[:, 0:8]), LDB, so_c[1])
-    dn_c = copy("s", T.dn[:, 128:256], T.bt[:, 0:512].indirect(T.so[:, 8:16]), so_c[3])
-    need("v", base, did("v", V.tensor_tensor(T.xu[:], T.li[:, 8:16], T.base[:], ADD)))
-    need("v", copy("v", T.bw[:, 0:512].indirect(T.uo[:, 0:16]), T.dn[:, 0:256], offsets(T.uo, T.xu, ho, 0)[3], dn_c))
+    oc = [offsets(T.oc, ho, 16 * (t // 2) + t % 2, t, 2) for t in range(4)]
+    dn_c = [copy("s", T.dn[:, 128 * u:128 * u + 128], T.bt[:, 0:512].indirect(T.oc[:, 16 * u:16 * u + 8]), LDB, oc[2 * u + 1])
+            for u in (0, 1)]
+    ol = [offsets(T.ol, hm, t, t, 4) for t in range(4)]
+    dn_l = copy("s", T.dn[:, 256:512], T.bt[:, 0:512].indirect(T.ol[:, 0:16]), ol[3])
+    for u in (0, 1):
+        x = copy("v", T.bw[:, 0:512].indirect(T.oc[:, 16 * u + 8:16 * u + 16]), T.dn[:, 128 * u:128 * u + 128],
+                 oc[2 * u + 1], x, dn_c[u])
+    need("v", x)
     b_c = did("v", V.quantize_mx(T.bq[:, 0:128], T.bsc[:, 0:128], T.bw[:, 0:512]))
 
     a_q = []
     for i in range(4):
-        need("v", ("lda%d" % (i // 2), 16))
+        need("v", ("lda%d" % (i // 3), 16))
         a_q.append(did("v", V.quantize_mx(T.aq[:, 128 * i:128 * i + 128], T.asc[:, 128 * i:128 * i + 128],
                                           T.at[:, 512 * i:512 * i + 512])))
-
-    bank_open = [False] * 8
 
     def own(i, half, bank, stop):
         need("t", a_q[i], b_c)
@@ -179,11 +181,11 @@ def rank_program(g, core, T, topo):
                                      T.bq[:, 128 * half:128 * half + 128], T.bsc[:, 128 * half:128 * half + 128],
                                      True, stop))
 
-    def unpack(b, col, bank, stop):
+    def unpack(b, col, bank, start, stop):
         c, s = E(b)
-        need("t", e_all)
+        need("t", e_all[0])
         return did("t", PE.matmul_mx(T.ps[:, 512 * bank:512 * bank + 128], c, s,
-                                     T.ex[:, col:col + 128], T.exs[:, col:col + 128], not bank_open[bank], stop))
+                                     T.ex[:, col:col + 128], T.exs[:, col:col + 128], start, stop))
 
     def ps(bank, lo, hi):
         return T.ps[:, 512 * bank + lo:512 * bank + hi]
@@ -191,40 +193,37 @@ def rank_program(g, core, T, topo):
     zc = [own(i, 0, i, True) for i in range(4)]
     for i in range(4):
         own(i, 0, 4 + i, False)
-        bank_open[4 + i] = True
-    cp = [copy("sssv"[i], T.zt[:, i:384:4], ps(i, UN, 128), zc[i]) for i in range(4)]
+    cp = [copy("s", T.zt[:, i:384:4], ps(i, UN, 128), zc[i]) for i in range(4)]
+    make_e(0)
+    make_e(1)
     need("v", *cp)
     zq_c = did("v", V.quantize_mx(T.zq[:, 0:128], T.zs[:, 0:128], T.zt[:, 0:512]))
 
     peers = [mine[(kr + 1 + j) % 4] for j in range(3)]
     sent = [0]
 
-    def cuts(en):
-        n = len(en)
-        return ([en[0:n // 4], en[n // 4:n // 2], en[n // 2:n]], [en[n // 2:3 * n // 4], en[3 * n // 4:n], en[0:n // 2]])
+    def put(dst_core, dst, src, name):
+        rid, pid = topo.addr(dst_core, core)
+        g.remote_dma(dst, src, sem[name], sem.ls, pid, rid, topo.mask(core, dst_core))
+        sent[0] += len(topo.engines(core, dst_core))
 
-    def sides(codes, col, o):
-        if codes:
-            return T.ex[:, o:o + UN].bitcast(dt.uint8), T.zq[:, col:col + UN].bitcast(dt.uint8)
-        return T.exs[:, o:o + UN], T.zs[:, col:col + UN]
+    def hop1(name, col, at):
+        for j in range(3):
+            o, c = SEC * (2 - j) + at, col + UN * j
+            put(peers[j], T.ex[:, o:o + UN].bitcast(dt.uint8), T.zq[:, c:c + UN].bitcast(dt.uint8), name + str(2 - j))
+            put(peers[j], T.exs[:, o:o + UN], T.zs[:, c:c + UN], name + str(2 - j))
 
-    def got(s):
-        c = cuts(topo.engines(mine[(kr + 1 + s) % 4], core))
-        return len(c[0][2 - s]) + len(c[1][2 - s])
+    def got(name, s):
+        return (name + str(s), 2 * len(topo.engines(mine[(kr + 1 + s) % 4], core)))
 
     need("g", zq_c)
-    for j in range(3):
-        rid, pid = topo.addr(peers[j], core)
-        for codes in (True, False):
-            dst, src = sides(codes, UN * j, SEC * (2 - j))
-            g.remote_dma(dst, src, sem["rc%d" % (2 - j)], sem.ls, pid, rid, topo.mask(core, peers[j]))
-            sent[0] += len(topo.engines(core, peers[j]))
+    hop1("rc", 0, 0)
 
-    so_l = offsets(T.so, T.li, hm, 16)[3]
-    dn_l = copy("s", T.dn[:, 256:512], T.bt[:, 0:512].indirect(T.so[:, 16:32]), so_l)
-    uo_l = offsets(T.uo, T.xu, hm, 16)[3]
-    need("v", copy("v", T.bw[:, 512:1024].indirect(T.uo[:, 16:32]), T.dn[:, 256:512], uo_l, dn_l))
+    need("v", copy("v", T.bw[:, 512:1024].indirect(T.ol[:, 16:32]), T.dn[:, 256:512], ol[3], dn_l))
     b_l = did("v", V.quantize_mx(T.bq[:, 128:256], T.bsc[:, 128:256], T.bw[:, 512:1024]))
+    did("v", V.memset(T.ct[:, 128:512], 0.0))
+    make_e(2)
+    make_e(3)
     need("t", b_l)
     zl = []
     for i in range(4):
@@ -234,75 +233,63 @@ def rank_program(g, core, T, topo):
     need("v", *lp)
     zq_l = did("v", V.quantize_mx(T.zq[:, 128:256], T.zs[:, 128:256], T.zt[:, 512:1024]))
     need("g", zq_l)
-    for codes in (True, False):
-        tr = []
-        for j in range(3):
-            dst, src = sides(codes, 128 + UN * j, SEC * (2 - j) + UN + 128)
-            en = cuts(topo.engines(core, peers[j]))[0 if codes else 1][j]
-            rid, pid = topo.addr(peers[j], core)
-            tr.append(RemoteDMATransfer(dst_ids=[DstId(rid=rid, pnc=pid)], dma_engine_mask=mask_of(en),
-                                        remote_sem=sem["rl%d" % (2 - j)], src=src, dst=dst))
-            sent[0] += len(en)
-        g.remote_dma_fused(tr, local_sem=sem.ls)
+    hop1("rl", 128, UN + 128)
+
+    need("v", LDU, c_all)
+    did("v", V.tensor_scalar(T.neg[:], T.up[:], 0, None, op0=LT))
+    did("v", V.tensor_scalar(T.pm[:], T.pidx[:], 15, None, op0=AND))
+    did("v", V.tensor_scalar(T.q4[:], T.pidx[:], 15, 2, op0=AND, op1=SHR))
+    did("v", V.tensor_scalar(T.p3[:], T.pidx[:], 3, None, op0=AND))
+    need("v", did("v", V.tensor_tensor(T.rb[:], T.rb[:], T.up[:], ADD)))
+    x = did("v", V.tensor_tensor(T.kc[:], T.kc[:], T.pm[:], ADD))
+    copy("v", T.q4f[:], T.q4[:])
+    need("v", x)
+    x = did("v", V.tensor_tensor(T.neg[:], T.neg[:], T.kc[:], MUL))
+    copy("v", T.p3f[:], T.p3[:])
+    need("v", x)
+    x = did("v", V.tensor_tensor(T.rb[:], T.rb[:], T.neg[:], ADD))
+    did("v", V.tensor_scalar(T.uc[:], T.uc[:], T.q4f[:, 0:1], None, op0=EQ))
+    need("v", x)
+    po = copy("v", T.po[:], T.rb[:])
 
     last = [None] * 4
     for s in (2, 1, 0):
-        need("t", ("rc%d" % s, 2 * len(topo.engines(mine[(kr + 1 + s) % 4], core))))
+        need("t", got("rc", s))
         for b in range(4):
-            last[b] = unpack(b, SEC * s, 4 + b, s == 0)
+            last[b] = unpack(b, SEC * s, 4 + b, False, s == 0)
     cc = [copy("svsv"[b], T.ct[:, b:128:4], ps(4 + b, 0, UN), last[b]) for b in range(4)]
     need("v", *cc)
     c_q = did("v", V.quantize_mx(T.cq[:], T.cs[:], T.ct[:]))
 
     far = other[kr]
-    rid, pid = topo.addr(far, core)
-    m = topo.mask(core, far)
     need("g", c_q)
-    g.remote_dma(T.ex[:, RX:RX + UN].bitcast(dt.uint8), T.cq[:, 0:UN].bitcast(dt.uint8), sem.rr, sem.ls, pid, rid, m)
-    g.remote_dma(T.exs[:, RX:RX + UN], T.cs[:, 0:UN], sem.rr, sem.ls, pid, rid, m)
-    sent[0] += 2 * len(topo.engines(core, far))
+    put(far, T.ex[:, RX:RX + UN].bitcast(dt.uint8), T.cq[:, 0:UN].bitcast(dt.uint8), "rr")
+    put(far, T.exs[:, RX:RX + UN], T.cs[:, 0:UN], "rr")
 
-    for i in range(4):
-        need("t", lp[i])
-        own(i, 1, i, False)
-        bank_open[i] = True
-    for s in range(3):
-        need("t", ("rl%d" % s, got(s)))
-        for b in range(4):
-            last[b] = unpack(b, SEC * s + 2 * UN, b, s == 2)
-    wl = [copy("s", T.wl[:, b:128:4], ps(b, 96, 128), last[b]) for b in range(4)]
-
-    need("v", LDU, c_all)
-    need("v", copy("v", T.up[32:64, :], T.up[0:32, :]))
-    copy("v", T.up[64:128, :], T.up[0:64, :])
-    did("v", V.tensor_scalar(T.pm[:], T.pidx[:], 15, None, op0=AND))
-    did("v", V.tensor_scalar(T.q4[:], T.pidx[:], 15, 2, op0=AND, op1=SHR))
-    need("v", did("v", V.tensor_scalar(T.p3[:], T.pidx[:], 3, None, op0=AND)))
-    copy("v", T.q4f[:], T.q4[:])
-    copy("v", T.p3f[:], T.p3[:])
-    did("v", V.tensor_scalar(T.neg[:], T.up[:], 0, None, op0=LT))
-    did("v", V.tensor_tensor(T.kc[:], T.kc[:], T.pm[:], ADD))
-    need("v", did("v", V.tensor_tensor(T.rb[:], T.rb[:], T.up[:], ADD)))
-    x = did("v", V.tensor_tensor(T.neg[:], T.neg[:], T.kc[:], MUL))
-    did("v", V.tensor_scalar(T.uc[:], T.uc[:], T.q4f[:, 0:1], None, op0=EQ))
-    need("v", x)
-    need("v", did("v", V.tensor_tensor(T.rb[:], T.rb[:], T.neg[:], ADD)))
-    need("v", copy("v", T.po[:], T.rb[:]))
+    need("v", po)
     need("v", copy("v", T.ix[:, 0:2 * H].indirect(T.po[:, 0:4]), T.sv[:]))
     need("v", did("v", V.tensor_tensor(T.ix[:], T.ix[:], T.uc[:], MUL)))
     need("v", did("v", V.tensor_tensor(T.i2[:], T.ix[:, 0:2 * H:2], T.ix[:, 1:2 * H:2], ADD)))
     need("v", did("v", V.tensor_tensor(T.i3[:], T.i2[:, 0:H:2], T.i2[:, 1:H:2], ADD)))
     fo = did("v", V.tensor_scalar(T.fo[:], T.i3[:], 4.0, T.p3f[:, 0:1], op0=MUL, op1=ADD))
+
+    for i in range(4):
+        need("t", lp[i])
+        own(i, 1, i, False)
+    for s in (2, 1, 0):
+        need("t", got("rl", s))
+        for b in range(4):
+            last[b] = unpack(b, SEC * s + 2 * UN, b, False, s == 0)
+    wl = [copy("s", T.wl[:, b:128:4], ps(b, 96, 128), last[b]) for b in range(4)]
     q = H // 4
     gl = copy("s", T.gl[:], T.wl[:, 0:136].indirect(T.fo[:, q * gm:q * gm + OC // 4]), fo, c_all, *wl)
 
     need("t", ("rr", 2 * len(topo.engines(far, core))))
     rc = []
     for b in range(4):
-        bank_open[4 + b] = False
         need("t", cc[b])
-        rc.append(unpack(b, RX, 4 + b, True))
-    wr = [copy("svsv"[b], T.wr[:, b:128:4], ps(4 + b, 0, UN), rc[b]) for b in range(4)]
+        rc.append(unpack(b, RX, 4 + b, True, True))
+    wr = [copy("v", T.wr[:, b:128:4], ps(4 + b, 0, UN), rc[b]) for b in range(4)]
     need("v", fo, gl, *wr)
     y = did("v", V.tensor_tensor(T.yt[:], T.wr[:, 0:136].indirect(T.fo[:, q * go:q * go + OC // 4]), T.gl[:], ADD))
     need("y", y)

from concourse.bass import DstId, RemoteDMATransfer
from concourse.mybir import dt, AluOpType, ActivationFunctionType

UN, OC = 32, 56
H = OC + UN
SEC = 2 * UN + 128
RX = 3 * SEC

SCRATCH = {
    "at": ("sbuf", [128, 2048], "bfloat16"),
    "bt": ("sbuf", [128, 512], "bfloat16"),
    "aq": ("sbuf", [128, 512], "float8_e4m3fn_x4"),
    "asc": ("sbuf", [128, 512], "uint8"),
    "bw": ("sbuf", [128, 1024], "bfloat16"),
    "bq": ("sbuf", [128, 256], "float8_e4m3fn_x4"),
    "bsc": ("sbuf", [128, 256], "uint8"),
    "dn": ("sbuf", [128, 512], "bfloat16"),
    "dg": ("sbuf", [128, 516], "bfloat16"),
    "one": ("sbuf", [128, 128], "bfloat16"),
    "ex": ("sbuf", [128, RX + 160], "float8_e4m3fn_x4"),
    "exs": ("sbuf", [128, RX + 160], "uint8"),
    "zt": ("sbuf", [128, 1024], "bfloat16"),
    "zq": ("sbuf", [128, 256], "float8_e4m3fn_x4"),
    "zs": ("sbuf", [128, 256], "uint8"),
    "ct": ("sbuf", [128, 512], "bfloat16"),
    "cq": ("sbuf", [128, 128], "float8_e4m3fn_x4"),
    "cs": ("sbuf", [128, 128], "uint8"),
    "li": ("sbuf", [128, 16], "int32"),
    "lx": ("sbuf", [128, 16], "int32"),
    "base": ("sbuf", [128, 16], "int32"),
    "oc": ("sbuf", [128, 32], "uint16"),
    "ol": ("sbuf", [128, 32], "uint16"),
    "up": ("sbuf", [128, 4], "int32"),
    "pidx": ("sbuf", [128, 4], "int32"),
    "pm": ("sbuf", [128, 4], "int32"),
    "kc": ("sbuf", [128, 4], "int32"),
    "rb": ("sbuf", [128, 4], "int32"),
    "neg": ("sbuf", [128, 4], "int32"),
    "po": ("sbuf", [128, 4], "uint16"),
    "q4": ("sbuf", [128, 4], "int32"),
    "q4f": ("sbuf", [128, 4], "float32"),
    "p3": ("sbuf", [128, 4], "int32"),
    "p3f": ("sbuf", [128, 4], "float32"),
    "sv": ("sbuf", [128, 2 * UN], "float32"),
    "uc": ("sbuf", [128, 2 * H], "float32"),
    "ix": ("sbuf", [128, 2 * H], "float32"),
    "i2": ("sbuf", [128, H], "float32"),
    "i3": ("sbuf", [128, H // 2], "float32"),
    "fo": ("sbuf", [128, H // 2], "uint16"),
    "wl": ("sbuf", [128, 136], "float32"),
    "wr": ("sbuf", [128, 136], "float32"),
    "gl": ("sbuf", [128, 224], "float32"),
    "yt": ("sbuf", [128, 224], "float32"),
    "ps": ("psum", [128, 4096], "float32"),
}
SEMAPHORES = ["v", "s", "t", "gp", "ldl", "ldb", "lda0", "lda1", "ldu", "st", "ls",
              "rc0", "rc1", "rc2", "rl0", "rl1", "rl2", "rr"]

ADD, MUL, AND, SHR, LT, EQ = (AluOpType.add, AluOpType.mult, AluOpType.bitwise_and, AluOpType.arith_shift_right,
                              AluOpType.is_lt, AluOpType.is_equal)
COPY = ActivationFunctionType.Copy


def rank_program(g, core, T, topo):
    rank = T.rank_of(core)
    if rank is None:
        return
    V, S, PE, SY = g.vector, g.scalar, g.tensor, g.sync
    sem = T.sem
    mine = [c for c in T.cores if topo.host(c) == topo.host(core)]
    other = [c for c in T.cores if topo.host(c) != topo.host(core)]
    kr = mine.index(core)
    hm = T.rank_of(mine[0])
    ho = T.rank_of(other[0])
    gm = 0 if topo.host(core) == topo.host(T.cores[0]) else 1
    go = 1 - gm

    tick = {"v": 0, "s": 0, "t": 0, "gp": 0}
    seen = {}

    def did(name, ins):
        ins.then_inc(sem[name], 1)
        tick[name] += 1
        return (name, tick[name])

    def need(qn, *ticks):
        q = {"v": V, "s": S, "t": PE, "g": g, "y": SY}[qn]
        for name, n in ticks:
            if seen.get((qn, name), 0) < n:
                seen[(qn, name)] = n
                q.wait_ge(sem[name], n)

    def copy(qn, out, in_, *ticks):
        need(qn, *ticks)
        return did(qn, S.activation(out, in_, COPY) if qn == "s" else V.tensor_copy(out, in_))

    def iota(out, pattern, base, cm=0, fl=False):
        return did("gp", g.iota(out, pattern, base, cm, allow_small_or_imprecise_dtypes=True) if fl
                   else g.iota(out, pattern, base, cm))

    def load_up(q, r):
        q.dma_start(T.up[r:r + 16, :], T.upl[:]).then_inc(sem.ldu, 16)

    for r in (0, 16):
        SY.dma_start(T.li[r:r + 16, 0:8], T.send[:]).then_inc(sem.ldl, 16)
        S.dma_start(T.li[r:r + 16, 8:16], T.un[:]).then_inc(sem.ldl, 16)
    S.dma_start(T.bt[:], T.b[:]).then_inc(sem.ldb, 16)
    load_up(SY, 0)
    SY.dma_start(T.at[:, 0:1536], T.a[:, 0:1536]).then_inc(sem.lda0, 16)
    load_up(S, 16)
    S.dma_start(T.at[:, 1536:2048], T.a[:, 1536:2048]).then_inc(sem.lda1, 16)
    need("y", ("lda1", 16))
    for r in range(32, 128, 16):
        load_up(SY, r)
    LDL, LDB, LDU = ("ldl", 64), ("ldb", 16), ("ldu", 128)

    z_bw = did("v", V.memset(T.bw[:, 0:512], 0.0))
    did("v", V.memset(T.one[:], 1.0))
    z_dg = did("v", V.memset(T.dg[:], 0.0))
    did("v", V.memset(T.zt[:, 384:512], 0.0))
    did("v", V.memset(T.zt[:, 896:1024], 0.0))
    b_base = iota(T.base[:, 8:16], [[UN, 4], [UN, 2]] if hm < ho else [[UN, 4], [-UN, 2]], -UN * kr - (UN if hm < ho else 0))
    b_zero = iota(T.base[:, 0:8], [[0, 8]], 0)
    iota(T.pidx[:], [[0, 4]], 0, 1)
    iota(T.kc[:], [[0, 2], [16, 2]], OC + 1)
    iota(T.rb[:], [[H, 2], [0, 2]], 0)
    need("g", z_dg)
    diag = did("gp", g.affine_select(T.dg[:, 3:515:4], T.one[:], [[-1, 128]], EQ, 0.0, 0, 1))
    iota(T.sv[:], [[0, 2], [1, UN]], 0, 0, True)
    iota(T.uc[:], [[0, H // 2], [1, 4]], 0, 0, True)
    iota(T.ix[:], [[0, 2 * H]], UN, 0, True)
    iota(T.wl[:, 128:136], [[0, 8]], 0, 0, True)
    c_all = iota(T.wr[:, 128:136], [[0, 8]], 0, 0, True)
    copy("s", T.bw[:, 512:1024], T.bw[:, 0:512], z_bw)

    need("v", b_base)
    did("v", V.tensor_scalar(T.base[:, 8:16], T.base[:, 8:16], 127, None, op0=AND))

    def E(b):
        o = SEC * b + UN
        return T.ex[:, o:o + 128], T.exs[:, o:o + 128]

    e_all = [None]

    def make_e(b):
        need("v", diag)
        c, s = E(b)
        e_all[0] = did("v", V.quantize_mx(c, s, T.dg[:, 3 - b:3 - b + 512]))

    need("v", LDL, b_zero)
    x = copy("v", T.li[32:64, :], T.li[0:32, :])
    need("v", x)
    for r in (0, 64):
        x = did("v", V.tensor_tensor(T.lx[r:r + 64, :], T.li[0:64, :], T.base[0:64, :], ADD))
    need("v", x)

    def offsets(out, h, at, t, k):
        return did("v", V.tensor_scalar(out[:, at:at + 7 * k + 1:k], T.lx[:, h:16:2], 4, t, op0=MUL, op1=ADD))

    oc = [offsets(T.oc, ho, 16 * (t // 2) + t % 2, t, 2) for t in range(4)]
    dn_c = [copy("s", T.dn[:, 128 * u:128 * u + 128], T.bt[:, 0:512].indirect(T.oc[:, 16 * u:16 * u + 8]), LDB, oc[2 * u + 1])
            for u in (0, 1)]
    ol = [offsets(T.ol, hm, t, t, 4) for t in range(4)]
    dn_l = copy("s", T.dn[:, 256:512], T.bt[:, 0:512].indirect(T.ol[:, 0:16]), ol[3])
    for u in (0, 1):
        x = copy("v", T.bw[:, 0:512].indirect(T.oc[:, 16 * u + 8:16 * u + 16]), T.dn[:, 128 * u:128 * u + 128],
                 oc[2 * u + 1], x, dn_c[u])
    need("v", x)
    b_c = did("v", V.quantize_mx(T.bq[:, 0:128], T.bsc[:, 0:128], T.bw[:, 0:512]))

    a_q = []
    for i in range(4):
        need("v", ("lda%d" % (i // 3), 16))
        a_q.append(did("v", V.quantize_mx(T.aq[:, 128 * i:128 * i + 128], T.asc[:, 128 * i:128 * i + 128],
                                          T.at[:, 512 * i:512 * i + 512])))

    def own(i, half, bank, stop):
        need("t", a_q[i], b_c)
        return did("t", PE.matmul_mx(T.ps[:, 512 * bank:512 * bank + 128],
                                     T.aq[:, 128 * i:128 * i + 128], T.asc[:, 128 * i:128 * i + 128],
                                     T.bq[:, 128 * half:128 * half + 128], T.bsc[:, 128 * half:128 * half + 128],
                                     True, stop))

    def unpack(b, col, bank, start, stop):
        c, s = E(b)
        need("t", e_all[0])
        return did("t", PE.matmul_mx(T.ps[:, 512 * bank:512 * bank + 128], c, s,
                                     T.ex[:, col:col + 128], T.exs[:, col:col + 128], start, stop))

    def ps(bank, lo, hi):
        return T.ps[:, 512 * bank + lo:512 * bank + hi]

    zc = [own(i, 0, i, True) for i in range(4)]
    for i in range(4):
        own(i, 0, 4 + i, False)
    cp = [copy("s", T.zt[:, i:384:4], ps(i, UN, 128), zc[i]) for i in range(4)]
    make_e(0)
    make_e(1)
    need("v", *cp)
    zq_c = did("v", V.quantize_mx(T.zq[:, 0:128], T.zs[:, 0:128], T.zt[:, 0:512]))

    peers = [mine[(kr + 1 + j) % 4] for j in range(3)]
    sent = [0]

    def put(dst_core, dst, src, name):
        rid, pid = topo.addr(dst_core, core)
        g.remote_dma(dst, src, sem[name], sem.ls, pid, rid, topo.mask(core, dst_core))
        sent[0] += len(topo.engines(core, dst_core))

    def hop1(name, col, at):
        for j in range(3):
            o, c = SEC * (2 - j) + at, col + UN * j
            put(peers[j], T.ex[:, o:o + UN].bitcast(dt.uint8), T.zq[:, c:c + UN].bitcast(dt.uint8), name + str(2 - j))
            put(peers[j], T.exs[:, o:o + UN], T.zs[:, c:c + UN], name + str(2 - j))

    def got(name, s):
        return (name + str(s), 2 * len(topo.engines(mine[(kr + 1 + s) % 4], core)))

    need("g", zq_c)
    hop1("rc", 0, 0)

    need("v", copy("v", T.bw[:, 512:1024].indirect(T.ol[:, 16:32]), T.dn[:, 256:512], ol[3], dn_l))
    b_l = did("v", V.quantize_mx(T.bq[:, 128:256], T.bsc[:, 128:256], T.bw[:, 512:1024]))
    did("v", V.memset(T.ct[:, 128:512], 0.0))
    make_e(2)
    make_e(3)
    need("t", b_l)
    zl = []
    for i in range(4):
        need("t", cp[i])
        zl.append(own(i, 1, i, True))
    lp = [copy("svsv"[i], T.zt[:, 512 + i:896:4], ps(i, 0, 96), zl[i]) for i in range(4)]
    need("v", *lp)
    zq_l = did("v", V.quantize_mx(T.zq[:, 128:256], T.zs[:, 128:256], T.zt[:, 512:1024]))
    need("g", zq_l)
    hop1("rl", 128, UN + 128)

    need("v", LDU, c_all)
    did("v", V.tensor_scalar(T.neg[:], T.up[:], 0, None, op0=LT))
    did("v", V.tensor_scalar(T.pm[:], T.pidx[:], 15, None, op0=AND))
    did("v", V.tensor_scalar(T.q4[:], T.pidx[:], 15, 2, op0=AND, op1=SHR))
    did("v", V.tensor_scalar(T.p3[:], T.pidx[:], 3, None, op0=AND))
    need("v", did("v", V.tensor_tensor(T.rb[:], T.rb[:], T.up[:], ADD)))
    x = did("v", V.tensor_tensor(T.kc[:], T.kc[:], T.pm[:], ADD))
    copy("v", T.q4f[:], T.q4[:])
    need("v", x)
    x = did("v", V.tensor_tensor(T.neg[:], T.neg[:], T.kc[:], MUL))
    copy("v", T.p3f[:], T.p3[:])
    need("v", x)
    x = did("v", V.tensor_tensor(T.rb[:], T.rb[:], T.neg[:], ADD))
    did("v", V.tensor_scalar(T.uc[:], T.uc[:], T.q4f[:, 0:1], None, op0=EQ))
    need("v", x)
    po = copy("v", T.po[:], T.rb[:])

    last = [None] * 4
    for s in (2, 1, 0):
        need("t", got("rc", s))
        for b in range(4):
            last[b] = unpack(b, SEC * s, 4 + b, False, s == 0)
    cc = [copy("svsv"[b], T.ct[:, b:128:4], ps(4 + b, 0, UN), last[b]) for b in range(4)]
    need("v", *cc)
    c_q = did("v", V.quantize_mx(T.cq[:], T.cs[:], T.ct[:]))

    far = other[kr]
    need("g", c_q)
    put(far, T.ex[:, RX:RX + UN].bitcast(dt.uint8), T.cq[:, 0:UN].bitcast(dt.uint8), "rr")
    put(far, T.exs[:, RX:RX + UN], T.cs[:, 0:UN], "rr")

    need("v", po)
    need("v", copy("v", T.ix[:, 0:2 * H].indirect(T.po[:, 0:4]), T.sv[:]))
    need("v", did("v", V.tensor_tensor(T.ix[:], T.ix[:], T.uc[:], MUL)))
    need("v", did("v", V.tensor_tensor(T.i2[:], T.ix[:, 0:2 * H:2], T.ix[:, 1:2 * H:2], ADD)))
    need("v", did("v", V.tensor_tensor(T.i3[:], T.i2[:, 0:H:2], T.i2[:, 1:H:2], ADD)))
    fo = did("v", V.tensor_scalar(T.fo[:], T.i3[:], 4.0, T.p3f[:, 0:1], op0=MUL, op1=ADD))

    for i in range(4):
        need("t", lp[i])
        own(i, 1, i, False)
    for s in (2, 1, 0):
        need("t", got("rl", s))
        for b in range(4):
            last[b] = unpack(b, SEC * s + 2 * UN, b, False, s == 0)
    wl = [copy("s", T.wl[:, b:128:4], ps(b, 96, 128), last[b]) for b in range(4)]
    q = H // 4
    gl = copy("s", T.gl[:], T.wl[:, 0:136].indirect(T.fo[:, q * gm:q * gm + OC // 4]), fo, c_all, *wl)

    need("t", ("rr", 2 * len(topo.engines(far, core))))
    rc = []
    for b in range(4):
        need("t", cc[b])
        rc.append(unpack(b, RX, 4 + b, True, True))
    wr = [copy("v", T.wr[:, b:128:4], ps(4 + b, 0, UN), rc[b]) for b in range(4)]
    need("v", fo, gl, *wr)
    y = did("v", V.tensor_tensor(T.yt[:], T.wr[:, 0:136].indirect(T.fo[:, q * go:q * go + OC // 4]), T.gl[:], ADD))
    need("y", y)
    SY.dma_start(T.y[:], T.yt[:]).then_inc(sem.st, 16)
    SY.wait_ge(sem.st, 16)
    g.wait_ge(sem.ls, sent[0])
    need("g", ("v", tick["v"]), ("s", tick["s"]), ("t", tick["t"]))
